import numpy as np, ml_dtypes
CORES = [6,15,38,47]
N = 4
BF = ml_dtypes.bfloat16
def gentries(a):
    return np.ascontiguousarray(a.reshape(8, 16, -1).transpose(0, 2, 1)).reshape(8, -1)
def gtable(e):
    e = np.asarray(e); return np.ascontiguousarray(e.reshape(8, -1, 16).transpose(0, 2, 1)).reshape(128, -1).astype(np.int32)
V, A, W, M, RO, ST = 2048, 256, 4096, 4096, 4, 1
H, E, Z = V - A, W - 1, M - 1
def parts(rng):
    a = rng.choice(np.array([1, 2, 4, 8]), (8, 16, 1)); b = rng.choice(np.array([15, 63, 255]), (8, 16, 1))
    e = rng.integers(-a, a + 1, (8, 16, W)); c = rng.integers(-b, b + 1, (8, 16, M)); m = rng.integers(0, M, (8, 2, W))
    share = rng.permutation(np.linspace(0.42, 0.7, 8)).reshape(8, 1, 1)
    k = np.where(rng.random((8, 2, M)) < share, rng.integers(0, E, (8, 2, M)), E)
    fill = rng.choice(np.array([0.9, 0.97, 1.0]), (N, 8, 1))
    p = np.where(rng.random((N, 8, V)) < fill, rng.integers(0, E, (N, 8, V)), E)
    return p, e, m, c, k
def lone(rng):
    return np.where(np.arange(2)[:, None] == rng.integers(0, 2, M), rng.integers(0, E, (2, M)), E)
def alike(x):
    return np.ascontiguousarray(np.broadcast_to(x, (N,) + x.shape))
def pack(p, e, m, c, k):
    e[:, :, E] = 0; m[:, :, E] = Z; k[:, :, Z] = E
    return {"todo": np.stack([gtable(a) for a in p]), "eff": alike(e.reshape(128, W).astype(np.float32).astype(BF)),
            "meth": alike((m[:, 0] + 4096 * m[:, 1]).astype(np.int32)), "pre": alike(c.reshape(128, M).astype(np.float32).astype(BF)),
            "kid": alike((k[:, 0] + 4096 * k[:, 1]).astype(np.int32))}
def setup_inputs(rng):
    return pack(*parts(rng))
def setup_inputs_room(rng):
    p, e, m, c, k = parts(rng)
    m = 3 * rng.integers(0, (M - 1) // 3, (8, 2, W)) + np.arange(W) % 3
    k = rng.integers(0, E, (8, 2, M)); one = rng.integers(0, 2, (8, M)); cl = np.arange(M) % 3
    k[:, 0] = np.where((cl == 0) | ((cl == 1) & (one == 0)), E, k[:, 0]); k[:, 1] = np.where((cl == 0) | ((cl == 1) & (one == 1)), E, k[:, 1])
    for q in range(N):
        for g in range(8):
            n = int(rng.choice(np.array([0, 1, H - 1, H, H + 1, V - 1, V, V + 1, 2 * V])))
            if q == 0: n = (V, V + 1, V - 1, H, H + 1, H - 1, 2 * V, 1)[g]
            n2 = int(rng.integers(max(0, n - V), n // 2 + 1)); n1 = n - 2 * n2; n0 = V - n1 - n2
            kinds = rng.permutation(np.repeat(np.array([0, 1, 2]), np.array([n0, n1, n2])))
            t = 3 * rng.integers(0, (W - 1) // 3, V) + kinds
            p[q, g] = np.where((kinds == 0) & (rng.random(V) < 0.3), E, t)
    return pack(p, e, m, c, k)
def setup_inputs_ties(rng):
    p, e, m, c, k = parts(rng)
    e[::2] = rng.integers(-1, 2, (4, 16, W)) * (rng.random((4, 16, W)) < 0.01)
    c[::2] = rng.integers(-2, 3, (4, 16, M))
    m[::2, 1] = np.where(rng.random((4, W)) < 0.3, m[::2, 0], m[::2, 1])
    m[1::2, 1] = m[1::2, 0] ^ 1
    c[1::2, :, 1::2] = c[1::2, :, 0::2]; i = int(rng.integers(0, 16))
    c[1::2, i, 1::2] = rng.integers(-255, 256, (4, M // 2))
    return pack(p, e, m, c, k)
def setup_inputs_ends(rng):
    p, e, m, c, k = parts(rng)
    e[0] = 8; e[1] = -8
    p[:, :2] = rng.integers(0, E, (N, 2, V)); m[:2] = rng.integers(0, Z, (2, 2, W)); c[:2] = rng.integers(-255, 256, (2, 16, M))
    k[0] = lone(rng); k[1] = lone(rng)
    c[2] = rng.choice(np.array([-255, 255, 0]), (16, M))
    p[:, 3] = rng.choice(np.array([0, 1, E - 1, E]), (N, V))
    m[4] = rng.choice(np.array([0, 1, M - 2, Z]), (2, W)); k[4][:, [0, 1, M - 2]] = rng.integers(0, E, (2, 3))
    k[5] = rng.choice(np.array([0, 1, E - 1, E]), (2, M))
    t = rng.permutation(E)[:2]; u = rng.permutation(Z)[:2]
    p[:, 6] = t[0]; m[6, 0, t[0]] = u[0]; m[6, 1, t[0]] = u[1]
    k[6, 0, u[0]] = t[0]; k[6, 1, u[0]] = t[1]; k[6, 0, u[1]] = t[1]; k[6, 1, u[1]] = E
    sg = rng.permutation(np.repeat(np.array([-1, 1]), 8))[:, None]
    e[7] = sg * 8 * (1 - 2 * (np.arange(W) % 2))
    p[:, 7] = 2 * rng.integers(0, E // 2, (N, V)) + (np.arange(N * V).reshape(N, V) >= N * V // 2 + 15)
    m[7, 0] = 2 * rng.integers(0, M // 2, W); m[7, 1] = 2 * rng.integers(0, M // 2 - 1, W) + 1; k[7] = lone(rng)
    lo = rng.integers(-255, 101, (16, M)); hi = rng.integers(-100, 256, (16, M))
    c[7] = np.where(np.arange(M) % 2 == 1, np.where(sg > 0, lo, -255), np.where(sg > 0, 255, hi))
    return pack(p, e, m, c, k)
def setup_inputs_thin(rng):
    p, e, m, c, k = parts(rng); p = rng.integers(0, E, (N, 8, V))
    fill = rng.choice(np.array([0.0, 0.02, 0.3, 1.0]), (N, 8, 1)); o = rng.permutation(8)
    fill[int(rng.integers(0, N))] = 0.0; fill[:, o[0]] = 0.0; fill[:, o[1:3]] = 1.0
    p = np.where(rng.random((N, 8, V)) < fill, p, E); p[:, o[3], :V // 2] = E
    g = int(o[4]); q = int(rng.integers(0, N - 1)); cl = np.arange(M) % 3
    m[g] = 3 * rng.integers(0, (M - 1) // 3, (2, W)) + np.arange(W) % 3
    one = np.arange(2)[:, None] == rng.integers(0, 2, M); leaf = 3 * rng.integers(0, E // 3, (2, M)); go = 3 * rng.integers(0, E // 3, (2, M)) + 2
    k[g] = np.where(cl == 1, leaf, np.where((cl == 2) & one, go, E))
    kinds = np.full(N, 2); kinds[[q - 1, q]] = 1
    p[:, g] = 3 * rng.integers(0, E // 3, (N, V)) + kinds[:, None]; p[(q + 2) % N, g] = E
    return pack(p, e, m, c, k)
def setup_inputs_spread(rng):
    p, e, m, c, k = parts(rng)
    o = np.stack([rng.permutation(E) for g in range(8)]); gi = np.arange(8)
    p = np.where(rng.random((N, 8, V)) < 0.97, o[gi[None, :, None], (E * rng.random((N, 8, V)) ** 4).astype(np.int64)], E)
    k = np.where(k == E, E, o[gi[:, None, None], (E * rng.random((8, 2, M)) ** 3).astype(np.int64)])
    s = rng.choice(np.array([-1, 1]), (8, 16, W)); e = s * np.minimum(8, np.floor(np.exp2(3.2 * rng.random((8, 1, W))) * rng.random((8, 16, W)) + 0.5)).astype(np.int64) * (rng.random((8, 1, W)) > 0.0625)
    s = rng.choice(np.array([-1, 1]), (8, 16, M)); c = s * np.minimum(255, np.floor(np.exp2(8 * rng.random((8, 16, M))))).astype(np.int64)
    w = int(rng.integers(0, 8)); a = rng.choice(np.array([-1, 1]), (16, 1)) * rng.integers(3, 8, (16, 1))
    e[w] = a * np.array([0, 1, -1])[np.arange(W) % 3] + rng.integers(-1, 2, (16, W)); c[w] = rng.integers(-127, 128, (16, M))
    m[w] = rng.integers(0, Z, (2, W)); k[w] = lone(rng)
    kinds = np.zeros((N, V), np.int64); kinds[0::2, V // 2:] = 1; kinds[1::2, :V // 2] = 2
    p[:, w] = 3 * rng.integers(0, E // 3, (N, V)) + kinds
    return pack(p, e, m, c, k)
def check_inputs(d):
    bad = []
    if np.min(d["todo"]) < 0 or np.max(d["todo"]) > E: bad.append("range of todo")
    for nm, hi in (("eff", 8), ("pre", 255)):
        x = np.asarray(d[nm]).astype(np.float32)
        if not np.all((x >= -hi) & (x <= hi) & (x == np.rint(x))): bad.append("whole numbers in range: " + nm)
    for nm, hi in (("meth", Z), ("kid", E)):
        x = np.asarray(d[nm]).astype(np.int64)
        if not np.all((x >= 0) & ((x & 4095) <= hi) & ((x >> 12) <= hi)): bad.append("range of " + nm)
    for nm in ("eff", "meth", "pre", "kid"):
        x = np.asarray(d[nm]).astype(np.float64)
        if not np.all(x == x[:1]): bad.append("not alike on all ranks: " + nm)
    if not np.all(np.asarray(d["eff"])[:, :, E].astype(np.float32) == 0): bad.append("effects of the empty type")
    if not np.all(np.asarray(d["meth"])[:, :, E] == Z + 4096 * Z): bad.append("methods of the empty type")
    if not np.all(np.asarray(d["kid"])[:, :, Z] == E + 4096 * E): bad.append("kids of the empty method")
    return bad
def reference(todo, eff, meth, pre, kid):
    p = np.stack([gentries(a) for a in todo]).astype(np.int64)
    ef = eff.astype(np.float32).astype(np.int64).reshape(N, 8, 16, W); pr = pre.astype(np.float32).astype(np.int64).reshape(N, 8, 16, M)
    me = meth.astype(np.int64); ki = kid.astype(np.int64)
    for rnd in range(RO):
        e = np.take_along_axis(ef, p[:, :, None, :], 3)
        line = np.ascontiguousarray(e.transpose(1, 2, 0, 3)).reshape(8, 16, N * V)
        st = (np.add.accumulate(line, axis=2) - line).reshape(8, 16, N, V).transpose(2, 0, 1, 3)
        m = np.take_along_axis(me, p, 2); m0 = m & 4095; m1 = m >> 12
        c0 = np.add.reduce((st >= np.take_along_axis(pr, m0[:, :, None, :], 3)).astype(np.int64), axis=2)
        c1 = np.add.reduce((st >= np.take_along_axis(pr, m1[:, :, None, :], 3)).astype(np.int64), axis=2)
        k = np.take_along_axis(ki, np.where(c1 > c0, m1, m0), 2)
        kk = np.stack([k & 4095, k >> 12], axis=-1).reshape(N, 8, 2 * V)
        row = np.full((N, 8, V), E, np.int64)
        for a in range(N):
            for g in range(8):
                v = kk[a, g][kk[a, g] != E][:V]; row[a, g, :len(v)] = v
        p = np.concatenate([np.roll(row[:, :, H:], 1, axis=0), row[:, :, :H]], axis=2)
    return {"yp": np.stack([gtable(a) for a in p]).astype(np.float32), "ys": np.ascontiguousarray(st.reshape(N, 128, V)[:, :, ::ST]).astype(np.float32)}

from concourse.bass import DstId, RemoteDMATransfer
from concourse.mybir import AluOpType as OP, AxisListType, ActivationFunctionType as AF

N, V, A, W, RO = 4, 2048, 256, 4096, 4
H16 = "float16"
CH = 224
NS = 544
SC = 704
RB = 4224
JB = 2 * RB
BIG = 16384
WW = JB + V + 16
RW = V + 16
SW = 2 * NS + 16
C1A = 200

SCRATCH = {}
for _names, _shape, _dt in (
        ("ef ep pr c0 c1 km kt k1", [128, W], "bfloat16"), ("mi ki ta tb", [128, 256], "int32"), ("ti", [128, 128], "int32"),
        ("lh", [128, 1024], "int32"), ("pt cm0 cm1 gg", [128, V], "bfloat16"), ("ml0 ml1", [128, 256], "uint16"),
        ("nat ofu", [128, 128], "uint16"), ("zz", [128, RW], "bfloat16"), ("msk", [128, 2 * CH], "bfloat16"),
        ("ea", [128, 16 + V], "bfloat16"), ("eb", [128, 16 + A], "bfloat16"), ("ls", [128, V], H16),
        ("yst", [128, V], "float32"), ("dh0 dh1", [128, V - SC], H16), ("df0", [128, SC], "float32"),
        ("cq", [128, SC], "bfloat16"), ("g32", [128, NS], "float32"), ("w0 w1", [128, WW], "bfloat16"),
        ("ws", [128, JB + 16 + NS], "float32"), ("wsb", [128, 2 * SW], "bfloat16"), ("rel off offm", [128, 16], "float32"),
        ("xs jcol", [128, 4], "float32"), ("jint", [128, 4], "int32"), ("rr", [128, 144], "bfloat16"),
        ("vt tt one idn idr idb same triu tril cj", [128, 128], "bfloat16"), ("nts", [128, 2, 128], "bfloat16"),
        ("wj of32", [128, 128], "float32"), ("yt id16 idm", [128, 128], H16), ("ypt", [128, 144], "float32"),
        ("bneg", [128, 8], "bfloat16"), ("seln", [128, 2, 8], "bfloat16"), ("sel0 sel1 sel2 sel3", [128, 8, 2], "bfloat16"),
        ("rl0 rl1 rl2 rl3", [128, 144], "uint16"), ("acc0 acc1 acc2 acc3", [128, 8], "float32"),
        ("lt0 lt1 lt2 lt3", [128, 24], "float32")):
    for _n in _names.split():
        SCRATCH[_n] = ("sbuf", _shape, _dt)
for _n in "pdt pnp pwp pp1 plp pdq".split():
    SCRATCH[_n] = ("psum", [128, 512], "float32")
SCRATCH["pnt"] = ("psum", [128, 4, 128], "float32")
SCRATCH["pct"] = ("psum", [128, 32, 16], "float32")

SEMAPHORES = (["cv", "cs", "ct", "cg", "dti", "dmi", "dki", "dpr", "def", "dpt", "dmv", "dyp", "dyq"]
              + ["dys%d" % i for i in range(3)] + ["dz%d" % r for r in range(RO)]
              + ["ent%d" % r for r in range(RO)] + ["tot%d" % r for r in range(RO)]
              + ["se%d" % r for r in range(RO)] + ["st%d" % r for r in range(RO)])
PSUM = [k for k in SCRATCH if SCRATCH[k][0] == "psum"]
ALL = 1 << 30


def emit(g, T, ops):
    queue = {"v": g.vector, "s": g.scalar, "t": g.tensor, "g": g, "y": g.sync}
    seen, deps, needed = {}, [], set()
    for i, o in enumerate(ops):
        d = set(o["after"])
        for acc, wr in ((o["r"], False), (o["w"], True)):
            for (nm, lo, hi) in acc:
                ps = nm in PSUM
                for (lo2, hi2, j, wr2) in seen.get(nm, []):
                    if ps or ((wr or wr2) and lo < hi2 and lo2 < hi):
                        d.add(j)
        for acc, wr in ((o["r"], False), (o["w"], True)):
            for (nm, lo, hi) in acc:
                lst = seen.setdefault(nm, [])
                if nm in PSUM:
                    lst[:] = [e for e in lst if ops[e[2]]["q"] != o["q"]]
                elif wr:
                    lst[:] = [e for e in lst if not (lo <= e[0] and e[1] <= hi)]
                lst.append((lo, hi, i, wr))
        d = [j for j in d if j != i and not (o["q"] == "t" and ops[j]["q"] == "t")
             and not (o["sem"] is not None and ops[j]["sem"] == o["sem"])]
        deps.append(d)
        if o["fn"] is not None:
            needed.update(d)
    total, token = {}, {}
    for i, o in enumerate(ops):
        if o["sem"] is not None:
            total[o["sem"]] = total.get(o["sem"], 0) + o["n"]
        elif i in needed:
            s = "c" + o["q"]
            total[s] = total.get(s, 0) + 1
            token[i] = (s, total[s])
    for i, o in enumerate(ops):
        if o["sem"] is not None:
            token[i] = (o["sem"], total[o["sem"]])
    waited = {}
    for i, o in enumerate(ops):
        if o["fn"] is None:
            continue
        want = {}
        for j in deps[i]:
            s, n = token[j]
            want[s] = max(want.get(s, 0), n)
        for s in sorted(want):
            if waited.get((o["q"], s), 0) < want[s]:
                queue[o["q"]].wait_ge(T.sem[s], want[s])
                waited[(o["q"], s)] = want[s]
        ins = o["fn"](queue[o["q"]])
        if o["dma"]:
            ins.then_inc(T.sem[o["sem"]], 16)
        elif o["sem"] is None and i in needed:
            ins.then_inc(T.sem[token[i][0]], 1)
    for s in sorted(total):
        if max([n for (q, s2), n in waited.items() if s2 == s] + [0]) < total[s]:
            g.wait_ge(T.sem[s], total[s])


def rank_program(g, core, T, topo):
    rank = T.rank_of(core)
    if rank is None:
        return
    ops = []

    def reg(x):
        return [(e, 0, ALL) if isinstance(e, str) else e for e in x]

    def op(q, fn, r, w, sem=None, n=0, dma=False, after=()):
        ops.append({"q": q, "fn": fn, "r": reg(r), "w": reg(w), "sem": sem, "n": n, "dma": dma, "after": list(after)})
        return len(ops) - 1

    def dma(out, in_, r, w, sem, after=()):
        return op("y", lambda e: e.dma_start(out, in_), r, w, sem, 16, True, after)

    def ts(out, in0, s1, s2, o0, o1, r, w):
        if o1 is None:
            return op("v", lambda e: e.tensor_scalar(out, in0, s1, None, o0), r, w)
        return op("v", lambda e: e.tensor_scalar(out, in0, s1, s2, o0, o1), r, w)

    def tt(out, in0, in1, o, r, w):
        return op("v", lambda e: e.tensor_tensor(out, in0, in1, o), r, w)

    def cp(out, in_, r, w):
        return op("v", lambda e: e.tensor_copy(out, in_), r, w)

    def ms(ap, c, w):
        return op("v", lambda e: e.memset(ap, c), [], w)

    def scan(out, d0, d1, init, o0, r, w):
        return op("v", lambda e: e.tensor_tensor_scan(out, d0, d1, init, o0, OP.add), r, w)

    def act(out, in_, f, r, w, **kw):
        return op("s", lambda e: e.activation(out, in_, f, **kw), r, w)

    def mm(out, lhsT, rhs, start, stop, r, w):
        return op("t", lambda e: e.matmul(out, lhsT, rhs, start, stop), r, w)

    def sel(out, in_, pat, cmp, fill, base, cm, r, w):
        return op("g", lambda e: e.affine_select(out, in_, pat, cmp, fill, base, cm), r, w)

    def const(out, n, c, w, step=0):
        return op("g", lambda e: e.iota(out, [[step, n]], c, 0, allow_small_or_imprecise_dtypes=True), [], w)

    def engines(src, dsts):
        m = topo.mask(T.cores[src], T.cores[dsts[0]])
        for d in dsts:
            m &= topo.mask(T.cores[src], T.cores[d])
        return m, bin(m).count("1")

    def send(src, dsts, aps, rsem, lsem, r):
        m, k = engines(rank, dsts)
        ids = [DstId(rid=topo.addr(T.cores[d])[0], pnc=topo.addr(T.cores[d])[1]) for d in dsts]
        tr = RemoteDMATransfer(dst_ids=ids, dma_engine_mask=m, remote_sem=T.sem[rsem], srcs=[src], dsts=aps)
        return op("g", lambda e: e.remote_dma_fused([tr], local_sem=T.sem[lsem]), r, [], lsem, k)

    def sums_to(src, rnd):
        if src < N - 1:
            return list(range(src + 1, N))
        return list(range(1, N - 1)) if rnd > 0 else []

    dma(T.mi[:], T.meth[:], [], ["mi"], "dmi")
    dma(T.ki[:], T.kid[:], [], ["ki"], "dki")
    dma(T.ti[:], T.todo[:], [], ["ti"], "dti")
    dma(T.pr[:], T.pre[:], [], ["pr"], "dpr")

    ms(T.zz[:], 0.0, ["zz"])
    ms(T.km[:, 0:V], 0.0, [("km", 0, V)])
    for h in range(2):
        act(T.ws[:, h * RB:h * RB + SW], T.zz[:, 0:SW], AF.Silu, ["zz"], [("ws", h * RB, h * RB + SW)])
    act(T.km[:, V:W], T.zz[:, 0:V], AF.Copy, ["zz"], [("km", V, W)])
    const(T.one[:], 128, 1, ["one"])
    sel(T.idn[:], T.one[:], [[-1, 128]], OP.is_equal, 0.0, 0, 1, ["one"], ["idn"])
    sel(T.same[:], T.one[:], [[-16, 8], [0, 16]], OP.is_ge, 0.0, 0, 1, ["one"], ["same"])
    sel(T.same[:], T.same[:], [[16, 8], [0, 16]], OP.is_ge, 0.0, 15, -1, ["same"], ["same"])
    op("g", lambda e: e.iota(T.jint[:, 0:1], [[0, 1]], 0, 1), [], ["jint"])
    sel(T.triu[:], T.same[:], [[-1, 128]], OP.is_ge, 0.0, 0, 1, ["same"], ["triu"])
    sel(T.tril[:], T.same[:], [[1, 128]], OP.is_gt, 0.0, 0, -1, ["same"], ["tril"])
    sel(T.idr[:], T.zz[:, 0:128], [[-1, 128]], OP.not_equal, float(RB), 0, 1, ["zz"], ["idr"])
    sel(T.idb[:], T.zz[:, 0:128], [[-1, 128]], OP.not_equal, float(-BIG), 0, 1, ["zz"], ["idb"])
    const(T.cj[:], 128, 0, ["cj"], 16)
    const(T.msk[:], 2 * CH, 1, ["msk"])
    sel(T.msk[:, 0:2 * CH:CH], T.zz[:, 0:2], [[0, 2]], OP.is_ge, 0.0, 0, 0, ["zz", "msk"], ["msk"])
    const(T.ea[:, 0:16], 16, 0, [("ea", 0, 16)])
    const(T.eb[:, 0:16], 16, 0, [("eb", 0, 16)])
    const(T.rr[:, 0:16], 16, 0, [("rr", 0, 16)])
    const(T.bneg[:], 8, -1, ["bneg"])
    sel(T.bneg[:], T.bneg[:], [[-16, 8]], OP.is_ge, 0.0, 0, 1, ["bneg"], ["bneg"])
    sel(T.bneg[:], T.bneg[:], [[16, 8]], OP.is_ge, 0.0, 15, -1, ["bneg"], ["bneg"])

    def weights(i):
        row, (wl, wh) = 8 * (i % 2), ((1.0, 1.0 / 16), (1.0 / 16, 16.0))[i // 2]
        nm = "sel%d" % i
        const(T[nm][:], 16, 0, [nm])
        sel(T[nm][:], T[nm][:], [[-16, 8], [-4, 2]], OP.not_equal, wl, -row, 1, [nm], [nm])
        sel(T[nm][:], T[nm][:], [[-16, 8], [-4, 2]], OP.not_equal, wh, -row - 1, 1, [nm], [nm])
        for r, x in ((2, wl), (3, wh), (4, -wl), (5, -wh)):
            sel(T[nm][:, :, 0], T[nm][:, :, 0], [[-16, 8]], OP.not_equal, x, -row - r, 1, [nm], [nm])

    weights(0)
    weights(1)
    const(T.seln[:], 16, 0, ["seln"])
    for r in (6, 7):
        sel(T.seln[:], T.seln[:], [[-8, 2], [-16, 8]], OP.not_equal, 1.0, -r, 1, ["seln"], ["seln"])
        sel(T.seln[:, 1, :], T.seln[:, 1, :], [[-16, 8]], OP.not_equal, -1.0, -r, 1, ["seln"], ["seln"])
    for h in range(2):
        const(T.w0[:, h * RB:h * RB + RW], RW, 0, [("w0", h * RB, h * RB + RW)])

    ts(T.ta[:], T.mi[:], W - 1, None, OP.bitwise_and, None, ["mi"], ["ta"])
    ts(T.tb[:], T.mi[:], 12, None, OP.logical_shift_right, None, ["mi"], ["tb"])
    cp(T.ml0[:], T.ta[:], ["ta"], ["ml0"])
    cp(T.ml1[:], T.tb[:], ["tb"], ["ml1"])
    for b, (sh, bits) in enumerate(((0, 255), (12, 255), (8, 15), (20, 15))):
        ts(T.lh[:, 256 * b:256 * b + 256], T.ki[:], sh, bits, OP.logical_shift_right, OP.bitwise_and, ["ki"], [("lh", 256 * b, 256 * b + 256)])
    ts(T.ta[:], T.ki[:], W - 1, None, OP.bitwise_and, None, ["ki"], ["ta"])
    ts(T.pt[:, 0:512], T.lh[:, 0:512], -16.0, 4080.0, OP.mult, OP.add, [("lh", 0, 512)], [("pt", 0, 512)])
    ts(T.pt[:, 1536:1792], T.ta[:], float(W - 1), None, OP.not_equal, None, ["ta"], [("pt", 1536, 1792)])
    ts(T.pt[:, 512:1024], T.lh[:, 512:1024], -16.0, 240.0, OP.mult, OP.add, [("lh", 512, 1024)], [("pt", 512, 1024)])
    tt(T.pt[:, 1024:1280], T.pt[:, 256:512], T.pt[:, 1536:1792], OP.mult, [("pt", 256, 512), ("pt", 1536, 1792)], [("pt", 1024, 1280)])
    tt(T.pt[:, 1280:1536], T.pt[:, 768:1024], T.pt[:, 1536:1792], OP.mult, [("pt", 768, 1024), ("pt", 1536, 1792)], [("pt", 1280, 1536)])
    ts(T.pt[:, 1792:2048], T.ki[:], float((W - 1) * W), None, OP.is_lt, None, ["ki"], [("pt", 1792, 2048)])
    for b, row in ((0, 0), (1, 2), (6, 6), (2, 1), (3, 3), (4, 4), (5, 5), (7, 7)):
        dma(T.km[row::16, :], T.pt[:, 256 * b:256 * b + 256], [("pt", 256 * b, 256 * b + 256)], ["km"], "dpt")
    dma(T.ef[:], T.eff[:], [], ["ef"], "def")

    def clear(rnd, after):
        wn = "w%d" % (rnd % 2)
        for h in range(2):
            dma(T[wn][:, h * RB:h * RB + RW], T.zz[:], ["zz"], [wn], "dz%d" % rnd, after)

    def table(q, dst, src, lst, a, b):
        r, w = [src, (lst, a, b)], [(dst, 16 * a, 16 * b)]
        o, i = T[dst][:, 16 * a:16 * b], T[src][:].indirect(T[lst][:, a:b])
        return cp(o, i, r, w) if q == "v" else act(o, i, AF.Copy, r, w)

    cp(T.nat[:], T.ti[:], ["ti"], ["nat"])
    ts(T.ta[:, 0:128], T.ti[:], 255, None, OP.bitwise_and, None, ["ti"], [("ta", 0, 128)])
    ts(T.ta[:, 128:256], T.ti[:], 8, None, OP.logical_shift_right, None, ["ti"], [("ta", 128, 256)])
    ts(T.tb[:, 0:128], T.ta[:, 0:128], 16.0, None, OP.mult, None, [("ta", 0, 128)], [("tb", 0, 128)])
    ts(T.jint[:, 1:2], T.jint[:, 0:1], 15, None, OP.bitwise_and, None, ["jint"], ["jint"])
    tt(T.tb[:, 128:256], T.tb[:, 0:128], T.ta[:, 128:256], OP.add, ["ta", ("tb", 0, 128)], [("tb", 128, 256)])
    ts(T.jcol[:, 0:1], T.jint[:, 1:2], float(JB), None, OP.add, None, ["jint"], ["jcol"])
    cp(T.rl0[:, 0:128], T.tb[:, 128:256], ["tb"], ["rl0"])
    ms(T.rel[:], 0.5, ["rel"])
    cp(T.id16[:], T.idn[:], ["idn"], ["id16"])
    ts(T.idm[:], T.idn[:], -1.0, None, OP.mult, None, ["idn"], ["idm"])
    table("s", "c0", "pr", "ml0", 0, 256)
    table("v", "c1", "pr", "ml1", 0, C1A)
    table("s", "k1", "km", "ml1", 0, 256)
    table("v", "kt", "km", "ml0", 0, 256)
    for row in range(8):
        dma(T.kt[8 + row::16, :], T.k1[row::16, :], ["k1"], ["kt"], "dmv")

    prev, nxt = (rank - 1) % N, (rank + 1) % N
    calls = [(0, 224), (224, 448), (448, 896), (896, 1344), (1344, 1792)]
    pieces = [(0, A)] + [(A + CH * k, A + CH * (k + 1)) for k in range(8)]

    for rnd in range(RO):
        fin = rnd == RO - 1
        rl, acc, lt, wn = "rl%d" % rnd, "acc%d" % rnd, "lt%d" % rnd, "w%d" % (rnd % 2)
        el, et = ("nat", "ef") if rnd == 0 else (rl, "ep")
        bcol = 5 if rnd == 0 else 6
        senders = [s for s in range(N) if rank in sums_to(s, rnd)]
        if senders:
            op(None, None, [], [lt], "tot%d" % rnd, sum(engines(s, sums_to(s, rnd))[1] for s in senders))
        mm(T.pdt[:, 0:128], T.zz[:, 0:128], T.zz[:, 0:128], True, False, ["zz"], ["pdt"])
        mm(T.pnt[:, 0:2, :], T.zz[:, 0:128], T.zz[:, 0:256], True, False, ["zz"], ["pnt"])

        def effects(dst, at, a, b, col):
            act(T[dst][:, 16 + at:16 + at + b - a], T[et][:].indirect(T[el][:, a // 16:b // 16]), AF.Copy,
                [et, (el, a // 16, b // 16)], [(dst, 16 + at, 16 + at + b - a), (acc, col, col + 1)],
                accum_out=T[acc][:, col:col + 1])

        def sums(c0, c1):
            to = sums_to(rank, rnd)
            if to:
                at = [6 * rank if rank < N - 1 else 6 * d for d in to]
                send(T[acc][:, c0:c1], to, [T[lt][:, a:a + c1 - c0] for a in at], "tot%d" % rnd, "st%d" % rnd, [(acc, c0, c1)])

        def states(a, b, src, at):
            n = b - a
            d0, o0 = (T.msk[:, 0:n], OP.mult) if n != A else (T.zz[:, 0:n], OP.add)
            scan(T.ls[:, a:b], d0, T[src][:, at:at + n], 0.0, o0, ["msk", "zz", (src, at, at + n)], [("ls", a, b)])

        def diff(k, a, b):
            if k == 1 and b <= SC:
                return
            dn, o = ("df%d" % k, a) if a < SC else ("dh%d" % k, a - SC)
            tt(T[dn][:, o:o + b - a], T["c%d" % k][:].indirect(T[rl][:, a // 16:b // 16]), T.ls[:, a:b], OP.subtract,
               ["c%d" % k, (rl, a // 16, b // 16), ("ls", a, b)], [(dn, o, o + b - a)])

        def look(q, dst, src, a, b):
            table(q, dst, src, rl, a // 16, b // 16)

        if rnd > 0:
            look("v", "cq", "c1", A, A + CH)
        if rnd > 0 and rank == N - 1:
            effects("ea", 0, A + calls[0][0], A + calls[0][1], 0)
            effects("ea", V - A, V, V + A, 5)
            sums(5, 6)
            for k in range(1, 5):
                effects("ea", calls[k][0], A + calls[k][0], A + calls[k][1], k)
        else:
            for k, (a, b) in enumerate(calls):
                effects("ea", a, A + a, A + b, k)
            if rnd == 0:
                effects("eb", 0, 0, A, 5)
            else:
                effects("ea", V - A, V, V + A, 5)
            sums(0, 6)
        if rnd == 0:
            table("s", "c1", "pr", "ml1", C1A, 256)
            for q in range(16):
                sel(T.ep[:, q::16], T.ef[:, 256 * q:256 * q + 256], [[0, 256]], OP.is_ge, 0.0, 0, 0, ["ef"], [("ep", q, q + 1)])
            weights(2)
            weights(3)
            look("s", "gg", "kt", 0, V)
            look("s", "cq", "c1", 0, A)
        else:
            look("s", "gg", "kt", A, A + 896)
            effects("eb", 0, 0, A, 6)
            look("s", "gg", "kt", 0, A)
            look("s", "gg", "kt", A + 896, V)
            look("s", "cq", "c1", 0, A)
            look("s", "cq", "c1", A + CH, SC)
        states(A, A + calls[0][1], "ea", 15)
        for k, (a, b) in enumerate(calls):
            diff(0, A + a, A + b)
            if k < 4:
                states(A + b, A + calls[k + 1][1], "ea", 15 + b)
            else:
                states(0, A, "eb", 15)
            if rnd > 0:
                diff(1, A + a, A + b)
        if rnd == 0:
            for a, b in calls:
                diff(1, A + a, A + b)
            look("v", "cq", "c1", A, SC)
        scan(T.rel[:, 2:9], T.ls[:, A + CH - 1:A + 7 * CH:CH], T.zz[:, 0:7], 0.5, OP.add, [("ls", A, V), "zz"], [("rel", 2, 9)])
        for q in range(16):
            mm(T.pnt[:, 0:2, q::16], T.gg[:, q::16], T.seln[:], False, q == 15, ["gg", "seln"], ["pnt"])
        for pb, a, b in (("plp", A + CH, SC), ("pdq", 0, A + CH)):
            mm(T[pb][:, 0:b - a], T.idn[:], T.cq[:, a:b], True, False, ["idn", ("cq", a, b)], [pb])
            mm(T[pb][:, 0:b - a], T.idm[:], T.ls[:, a:b], False, True, ["idm", ("ls", a, b)], [pb])
        own = None
        if rank == 0 or rnd == 0:
            own = bcol
        elif rank == N - 1:
            own = 5
        if senders:
            got = T[lt][:, 0:6 * rank + (1 if N - 1 in senders else 0)]
            op("v", lambda e, got=got: e.tensor_reduce(T.xs[:, 0:1], got, AxisListType.X, OP.add), [lt], ["xs"])
        ts(T.rel[:, 0:1], T[acc][:, bcol:bcol + 1], -1.0, 0.5, OP.mult, OP.add, [(acc, bcol, bcol + 1)], [("rel", 0, 1)])
        if not senders:
            offs = ts(T.off[:, 0:9], T.rel[:, 0:9], T[acc][:, own:own + 1], None, OP.add, None, ["rel", acc], ["off"])
        elif own is None:
            offs = ts(T.off[:, 0:9], T.rel[:, 0:9], T.xs[:, 0:1], None, OP.add, None, ["rel", "xs"], ["off"])
        else:
            offs = ts(T.off[:, 0:9], T.rel[:, 0:9], T.xs[:, 0:1], T[acc][:, own:own + 1], OP.add, OP.add, ["rel", "xs", acc], ["off"])
        diff(0, 0, A)
        if not fin:
            clear(rnd + 1, [offs])
        for k in range(2):
            cm = "cm%d" % k
            for i in (1, 2, 0, 3, 4, 5, 6, 7, 8):
                a, b = pieces[i]
                if a < SC:
                    pb, at = ("df0", a) if k == 0 else ("pdq", a) if i < 2 else ("plp", 0)
                    act(T[cm][:, a:b], T[pb][:, at:at + b - a], AF.Sign, [(pb, at, at + b - a), "off"], [(cm, a, b)],
                        bias=T.off[:, i:i + 1], scale=-1.0)
                else:
                    ts(T[cm][:, a:b], T["dh%d" % k][:, a - SC:b - SC], T.off[:, i:i + 1], None, OP.is_le, None,
                       [("dh%d" % k, a - SC, b - SC), "off"], [(cm, a, b)])
            for q in range(16):
                mm(T.pdt[:, q:128:16], T[cm][:, q::16], T.same[:, 0:128:16] if k else T.bneg[:], False, k == 1 and q == 15,
                   [cm, "same", "bneg"], ["pdt"])
        act(T.nts[:], T.pnt[:, 0:2, :], AF.Copy, ["pnt"], ["nts"])
        mm(T.pnp[:, 0:128], T.nts[:, 0, :], T.idn[:], True, False, ["nts", "idn"], ["pnp"])
        mm(T.pwp[:, 0:128], T.idn[:], T.cj[:], True, False, ["idn", "cj"], ["pwp"])
        mm(T.pwp[:, 0:128], T.nts[:, 0, :], T.idb[:], False, False, ["nts", "idb"], ["pwp"])
        act(T.g32[:], T.gg[:, 0:NS], AF.Copy, [("gg", 0, NS)], ["g32"])
        ts(T.vt[:], T.pdt[:, 0:128], 0.0, None, OP.is_gt, None, ["pdt"], ["vt"])
        mm(T.pp1[:, 0:128], T.vt[:], T.idr[:], True, False, ["vt", "idr"], ["pp1"])
        tt(T.tt[:], T.vt[:], T.nts[:, 1, :], OP.mult, ["vt", "nts"], ["tt"])
        mm(T.pnp[:, 0:128], T.tt[:], T.idn[:], False, True, ["tt", "idn"], ["pnp"])
        mm(T.pwp[:, 0:128], T.tt[:], T.idb[:], False, True, ["tt", "idb"], ["pwp"])
        scan(T.rr[:, 16:144], T.pnp[:, 0:128], T.zz[:, 0:128], 0.0, OP.add, ["pnp", "zz"], [("rr", 16, 144)])
        act(T.wj[:], T.pwp[:, 0:128], AF.Identity, ["pwp", "jcol"], ["wj"], bias=T.jcol[:, 0:1])
        mm(T.pp1[:, 0:128], T.tril[:], T.rr[:, 16:144], False, False, ["tril", "rr"], ["pp1"])
        mm(T.pp1[:, 0:128], T.triu[:], T.rr[:, 15:143], False, True, ["triu", "rr"], ["pp1"])
        mm(T.pct[:, 0:8, :], T.zz[:, 0:128], T.zz[:, 0:128], True, False, ["zz"], ["pct"])
        tt(T.of32[:], T.pp1[:, 0:128], T.wj[:], OP.max, ["pp1", "wj"], ["of32"])
        ts(T.ofu[:], T.of32[:], 16.0, None, OP.add, None, ["of32"], ["ofu"])
        cp(T[wn][:].indirect(T.ofu[:, NS // 16:128]), T.gg[:, NS:V], ["ofu", "gg"], [wn])
        banks = ("plp", "pdq", "pdt", "pnp", "pwp")
        if fin:
            for i in range(5):
                a, b = pieces[2 * i][0], pieces[min(2 * i + 1, 8)][1]
                mm(T[banks[i]][:, 0:b - a], T.id16[:], T.ls[:, a:b], True, True, ["id16", ("ls", a, b)], [banks[i]])

        def fold(src, base, m, stop):
            for h in range(2):
                sn, b = "sel%d" % (h + (2 if fin else 0)), base[h]
                for d in range(-1, 16):
                    lhs = T[src][:, b + 16 + d:b + 16 + d + 16 * m - 15:16]
                    if d == -1:
                        o, rhs = T.pct[0:m, 0:8, 0], T[sn][:, :, 1]
                    elif d == 15:
                        o, rhs = T.pct[0:m, 0:8, 15], T[sn][:, :, 0]
                    else:
                        o, rhs = T.pct[0:m, 0:8, d:d + 2], T[sn][:]
                    mm(o, lhs, rhs, False, stop and h == 1 and d == 15, [(src, b, b + 16 * m + 16), sn], ["pct"])

        act(T.ws[:].indirect(T.ofu[:, 0:NS // 16]), T.g32[:], AF.Silu, ["ofu", "g32"], ["ws"])
        for h in range(2):
            act(T.wsb[:, h * SW:(h + 1) * SW], T.ws[:, h * RB:h * RB + SW], AF.Copy, ["ws"], [("wsb", h * SW, (h + 1) * SW)])
        fold("wsb", (0, SW), NS // 8, False)
        if not fin:
            for h in range(2):
                act(T.ws[:, h * RB:h * RB + SW], T.zz[:, 0:SW], AF.Copy, ["zz"], [("ws", h * RB, h * RB + SW)])
        else:
            act(T.offm[:, 0:9], T.off[:, 0:9], AF.Identity, ["off"], ["offm"], bias=-0.5)
            for k, (i0, i1) in enumerate(((0, 4), (4, 7), (7, 9))):
                for i in range(i0, i1):
                    a, b = pieces[i]
                    at = a - pieces[i - i % 2][0]
                    act(T.yst[:, a:b], T[banks[i // 2]][:, at:at + b - a], AF.Identity, [banks[i // 2], "offm"], [("yst", a, b)],
                        bias=T.offm[:, i:i + 1])
                a, b = pieces[i0][0], pieces[i1 - 1][1]
                dma(T.ys[:, a:b], T.yst[:, a:b], [("yst", a, b)], [], "dys%d" % k)
        fold(wn, (0, RB), 128, True)
        ts(T.yt[:], T.pct[:, 0:8, :], -1.0, 2047.0, OP.mult, OP.add, ["pct"], ["yt"])
        mm(T.plp[:, 0:128], T.yt[:], T.id16[:], True, True, ["yt", "id16"], ["plp"])
        nb = "ypt" if fin else "rl%d" % (rnd + 1)
        ts(T[nb][:, 16:144], T.plp[:, 0:128], 2048.0, None, OP.add, None, ["plp"], [(nb, 16, 144)])
        send(T[nb][:, 128:144], [nxt], [T[nb][:, 0:16]], "ent%d" % rnd, "se%d" % rnd, [(nb, 128, 144)])
        op(None, None, [], [(nb, 0, 16)], "ent%d" % rnd, engines(prev, [rank])[1])
        if fin:
            dma(T.yp[:, 16:128], T.ypt[:, 16:128], [("ypt", 16, 128)], [], "dyp")
            dma(T.yp[:, 0:16], T.ypt[:, 0:16], [("ypt", 0, 16)], [], "dyq")
    emit(g, T, ops)
